import numpy as np
import ml_dtypes


def mxq(x, axis, fmt="e4m3"):
    dtype, down = {"e4m3": (ml_dtypes.float8_e4m3fn, 7), "e5m2": (ml_dtypes.float8_e5m2, 14)}[fmt]
    v = np.moveaxis(np.asarray(x, np.float32).astype(ml_dtypes.bfloat16).astype(np.float64), axis, -1)
    blocks = v.reshape(v.shape[:-1] + (-1, 32))
    amax = np.abs(blocks).max(-1, keepdims=True)
    byte = np.maximum(np.where(amax > 0, np.frexp(amax)[1] - 1 + 127, 0) - down, 1)
    scale = np.exp2(byte - 127.0)
    codes = (blocks / scale).astype(np.float32).astype(dtype).astype(np.float64)
    return np.moveaxis((codes * scale).reshape(v.shape), -1, axis)


WIDE = False


def mx_kscale(k):
    if not WIDE:
        return np.ones(k)
    levels = np.array([10, -10, 5, -5, 0])
    if k % 512:
        return np.exp2(np.random.permutation(np.resize(levels, k // 32))).repeat(32)
    a = np.empty((k // 512, 16))
    for p in range(k // 512):
        a[p, :8] = np.random.permutation(np.resize(levels, 8))
        for g in range(8):
            far = levels[np.abs(levels - a[p, g]) >= 10]
            a[p, g + 8] = far[np.random.randint(len(far))]
    return np.exp2(a.ravel()).repeat(32)


def f64(x):
    return np.asarray(x).astype(np.float64)


def striped(idx):
    return np.tile(np.asarray(idx).reshape(-1, 16).T, (8, 1)).astype(np.uint16)


def unstriped(offs):
    return offs[:16].T.reshape(-1).astype(np.int64)


E2M1 = np.array([0.0, 0.5, 1.0, 1.5, 2.0, 3.0, 4.0, 6.0, -0.0, -0.5, -1.0, -1.5, -2.0, -3.0, -4.0, -6.0])


def pack_weight(w, fmt):
    k, n = w.shape
    w = f64(np.asarray(w, np.float32).astype(ml_dtypes.bfloat16)).reshape(k // 32, 32, n)
    amax = np.abs(w).max(1)
    if fmt == "e4m3":
        byte = np.frexp(amax)[1] - 1 + 127 - 7
    else:
        mant, ex = np.frexp(amax / 6.0)
        byte = np.where(mant > 0.5, ex, ex - 1) + 127
    byte = np.clip(np.where(amax > 0, byte, 1), 1, 254)
    scaled = (w * np.exp2(127.0 - byte)[:, None, :]).reshape(k, n).astype(np.float32)
    by_word = np.ascontiguousarray(scaled.reshape(k // 512, 128, 4, n).transpose(0, 1, 3, 2))
    if fmt == "e4m3":
        words = by_word.astype(ml_dtypes.float8_e4m3fn).view(np.uint8)
    else:
        c = by_word.astype(ml_dtypes.float4_e2m1fn).view(np.uint8) & 0xF
        words = (c[..., 0::2] | (c[..., 1::2] << 4)).reshape(k // 512, 128, 2 * n)
    return np.ascontiguousarray(words), np.ascontiguousarray(byte.astype(np.uint8).reshape(k // 512, 16, n))


def unpack_weight(words, scales, fmt):
    g, _, n = scales.shape
    words = np.ascontiguousarray(words).reshape(g, 128, n, -1)
    if fmt == "e4m3":
        vals = words.view(ml_dtypes.float8_e4m3fn).astype(np.float64)
    else:
        nib = np.empty((g, 128, n, 4), np.uint8)
        nib[..., 0::2] = words & 0xF
        nib[..., 1::2] = words >> 4
        vals = E2M1[nib]
    vals = vals * np.repeat(np.exp2(scales.astype(np.float64) - 127.0), 8, axis=1)[..., None]
    return vals.transpose(0, 1, 3, 2).reshape(g * 512, n)


B, N, T, D, DV, NQ = 2, 512, 2048, 1024, 128, 256


def setup_inputs():
    n = np.random.standard_normal
    seg = T // B
    idx = np.concatenate([b * seg + np.random.permutation(seg)[:N] for b in range(B)])
    s = mx_kscale(D)[:, None]
    u = np.ones(T)
    u[idx] = mx_kscale(B * N)
    r = np.random.uniform(0.5, 2.0, T)
    k = n((D, T)) / s
    v = n((DV, T)) / (u * r)
    kp = pack_weight(k, "e4m3")
    return {
        "qT": (n((B, D, NQ)) * s * (1.00 / np.sqrt(D))).astype(np.float32),
        "k_words": kp[0],
        "k_scales": kp[1],
        "vT": v.astype(np.float32),
        "vs": np.tile(u * r, (128, 1)).astype(np.float32),
        "kb": np.tile(n(T), (128, 1)).astype(np.float32),
        "og": n((B, NQ, DV)).astype(np.float32),
        "offs": striped(idx),
    }


def reference(qT, k_words, k_scales, vT, vs, kb, og, offs):
    idx = unstriped(offs)
    k = unpack_weight(k_words, k_scales, "e4m3")
    v = f64(vT)
    pick = lambda x: x[:, idx].reshape(x.shape[0], B, N).transpose(1, 0, 2)
    q = f64(qT)
    score = mxq(q, 1, "e4m3").transpose(0, 2, 1) @ pick(k)
    score = score + pick(f64(kb))[:, :1, :]
    p = 1.0 / (1.0 + np.exp(-score))
    w = p * pick(f64(vs))[:, :1, :]
    y = mxq(w, 2, "e4m3") @ mxq(pick(v).transpose(0, 2, 1), 1, "e4m3")
    y = y / 16.0
    y = y / (1.0 + np.exp(-f64(og)))
    return y

@@ -1,0 +1,189 @@
+from contextlib import ExitStack
+
+import concourse.mybir as mybir
+from concourse.masks import make_identity
+
+B, N, T, D, DV, NQ = 2, 512, 2048, 1024, 128, 256
+FLOPS = 2 * B * NQ * N * (D + DV)
+
+F32 = mybir.dt.float32
+BF16 = mybir.dt.bfloat16
+I32 = mybir.dt.int32
+U32 = mybir.dt.uint32
+U16 = mybir.dt.uint16
+U8 = mybir.dt.uint8
+FP8X4 = mybir.dt.float8_e4m3fn_x4
+ACT = mybir.ActivationFunctionType
+ALU = mybir.AluOpType
+
+P = 128
+PACK = 4
+PASSES = D // (P * PACK)
+SEG = T // B
+RUN = 8
+LIST_COLS = N // 16
+LAST = P - 1
+LOADED = 127
+HALVES = NQ // P
+
+
+def tile_attend_sigm_kb_gate_segb2q256n512t2048_kernel(tc, qT, k_words, k_scales, vT, vs, kb, og, offs, out):
+    nc = tc.nc
+    with ExitStack() as ctx:
+        sb = ctx.enter_context(tc.tile_pool(name="sb", bufs=1))
+        ps = ctx.enter_context(tc.psum_pool(name="ps", bufs=1))
+
+        offsets = sb.tile([P, B * LIST_COLS], U16, name="offsets")
+        nc.sync.dma_start(offsets[:], offs)
+
+        def seq_list(b):
+            return offsets[:, b * LIST_COLS : (b + 1) * LIST_COLS]
+
+        scale_pool = sb.tile([P, T], U8, name="scale_pool", align_bytes=64)
+        kb_pool = sb.tile([P, T], F32, name="kb_pool")
+        vs_pool = sb.tile([P, T], F32, name="vs_pool")
+        nc.gpsimd.memset(scale_pool[:].bitcast(I32), 0)
+        nc.vector.memset(kb_pool[0:LOADED, :].bitcast(I32), 0)
+        nc.vector.memset(vs_pool[0:LOADED, :].bitcast(I32), 0)
+        nc.sync.dma_start(kb_pool[LOADED:P, :], kb[LOADED:P, :])
+        nc.sync.dma_start(vs_pool[LOADED:P, :], vs[LOADED:P, :])
+        for quad in range(4):
+            nc.sync.dma_start(
+                scale_pool[32 * quad : 32 * quad + 4 * PASSES, :].bitcast(I32),
+                k_scales[:, 4 * quad : 4 * quad + 4, :].bitcast(I32),
+            )
+
+        v_raw = [sb.tile([P, SEG], F32, name=f"v_raw{b}", tag=f"v_raw{b}") for b in range(B)]
+        for b in range(B):
+            nc.sync.dma_start(v_raw[b][:], vT[:, b * SEG : (b + 1) * SEG])
+        word_pool = [sb.tile([P, T], I32, name=f"word_pool{o}") for o in range(PASSES)]
+        q_raw = [[sb.tile([P, PACK, NQ], F32, name=f"q_raw{b}{o}") for o in range(PASSES)] for b in range(B)]
+        for b in range(B):
+            for o in range(PASSES):
+                rows = qT[b, o * P * PACK : (o + 1) * P * PACK, :]
+                nc.sync.dma_start(q_raw[b][o][:], rows.rearrange("(p j) q -> p j q", j=PACK))
+        for b in range(B):
+            for o in range(PASSES):
+                words = k_words[o].rearrange("p t r -> p (t r)").bitcast(I32)
+                nc.sync.dma_start(word_pool[o][:, b * SEG : (b + 1) * SEG], words[:, b * SEG : (b + 1) * SEG])
+        og_raw = sb.tile([P, B * HALVES, DV], F32, name="og_raw")
+        nc.sync.dma_start(og_raw[:], og.rearrange("b (h p) e -> p (b h) e", p=P))
+
+        ident_f32 = sb.tile([P, P], F32, name="ident_f32")
+        ident_bf16 = sb.tile([P, P], BF16, name="ident_bf16")
+        make_identity(nc, ident_bf16[:])
+        make_identity(nc, ident_f32[:])
+
+        def token_columns(pool_tile, label, tag):
+            picked = sb.tile([P, PACK, B * P], F32, name=f"{label}_picked")
+            dealt = picked[:].bitcast(U32).rearrange("p r (m i) -> p m r i", i=RUN)
+            nc.vector.tensor_copy(dealt, pool_tile[:].bitcast(U32).indirect(offsets[:]))
+            cols = []
+            for b in range(B):
+                turned = ps.tile([P, PACK, P], F32, name=f"{label}_turned{b}", tag=f"{tag}{b}")
+                for r in range(PACK):
+                    nc.tensor.transpose(turned[:, r, :], picked[:, r, b * P : (b + 1) * P], ident_f32[:])
+                cols.append(turned[:, :, LAST])
+            return cols
+
+        kb_turned = token_columns(kb_pool, "kb", "scores")
+        vs_cols = token_columns(vs_pool, "vs", "vs_bank")
+
+        scale_picked = sb.tile([P, B * N], U8, name="scale_picked", align_bytes=64)
+        nc.vector.tensor_copy(scale_picked[:], scale_pool[:].indirect(offsets[:]))
+        k_planes = sb.tile([P, PACK, B * P], U8, name="k_planes", align_bytes=64)
+        nc.vector.tensor_copy(
+            k_planes[:].bitcast(I32).rearrange("p r (m w) -> p m r w", w=RUN // 4),
+            scale_picked[:].bitcast(I32).rearrange("p (m r w) -> p m r w", r=PACK, w=RUN // 4),
+        )
+
+        v_pool = sb.tile([P, T], BF16, name="v_pool", align_bytes=64)
+        v_turned = ps.tile([P, B, PACK, DV], BF16, name="v_turned")
+        v_woven = sb.tile([P, B, DV, PACK], BF16, name="v_woven", align_bytes=64)
+        for b in range(B):
+            nc.scalar.activation(v_pool[:, b * SEG : (b + 1) * SEG], v_raw[b][:], ACT.Copy)
+            v_picked = sb.tile([P, PACK, P], BF16, name=f"v_picked{b}", align_bytes=64)
+            nc.scalar.activation(
+                v_picked[:].rearrange("p r (m i) -> p m r i", i=RUN),
+                v_pool[:, : (b + 1) * SEG].indirect(seq_list(b)),
+                ACT.Copy,
+            )
+            for r in range(PACK):
+                nc.tensor.transpose(v_turned[:, b, r, :], v_picked[:, r, :], ident_bf16[:])
+        kb_cols = sb.tile([P, B, PACK], F32, name="kb_cols", tag="v_raw1")
+        for b in range(B):
+            nc.scalar.activation(kb_cols[:, b, :], kb_turned[b], ACT.Copy)
+        nc.scalar.copy(v_woven[:], v_turned[:].rearrange("p b r e -> p b e r"))
+        v_codes = sb.tile([P, B * DV], U32, name="v_codes", align_bytes=64)
+        v_planes = sb.tile([P, B * DV], U8, name="v_planes", align_bytes=64)
+        nc.vector.quantize_mx(v_codes[:].bitcast(FP8X4), v_planes[:], v_woven[:].rearrange("p b e r -> p (b e r)"))
+
+        gate = sb.tile([P, B * HALVES, DV], F32, name="gate")
+        y_bank = ps.tile([P, B * HALVES, DV], F32, name="y_bank")
+
+        probs = []
+        for b in range(B):
+            q_codes, q_planes, keys = [], [], []
+            for o in range(PASSES):
+                q_woven = sb.tile([P, NQ, PACK], BF16, name=f"q_woven{b}{o}", align_bytes=64)
+                nc.scalar.copy(
+                    q_woven[:].rearrange("p (c i) j -> p c j i", i=4),
+                    q_raw[b][o][:].rearrange("p j (c i) -> p c j i", i=4),
+                )
+                codes = sb.tile([P, NQ], U32, name=f"q_codes{b}{o}", align_bytes=64)
+                planes = sb.tile([P, NQ], U8, name=f"q_planes{b}{o}", align_bytes=64)
+                nc.vector.quantize_mx(codes[:].bitcast(FP8X4), planes[:], q_woven[:].rearrange("p q j -> p (q j)"))
+                q_codes.append(codes)
+                q_planes.append(planes)
+            for o in range(PASSES):
+                picked = sb.tile([P, PACK, P], U32, name=f"keys{b}{o}", align_bytes=64)
+                nc.vector.tensor_copy(
+                    picked[:].rearrange("p r (m i) -> p m r i", i=RUN),
+                    word_pool[o][:, : (b + 1) * SEG].bitcast(U32).indirect(seq_list(b)),
+                )
+                keys.append(picked)
+            scores = [ps.tile([P, NQ], F32, name=f"scores{b}{r}", tag=f"scores{r}") for r in range(PACK)]
+            for o in range(PASSES):
+                for r in range(PACK):
+                    nc.tensor.matmul_mx(
+                        scores[r][:],
+                        lhsT=keys[o][:, r, :].bitcast(FP8X4),
+                        lhsT_scale=k_planes[4 * o :, r, b * P : (b + 1) * P],
+                        rhs=q_codes[o][:].bitcast(FP8X4),
+                        rhs_scale=q_planes[o][:],
+                        start=(o == 0),
+                        stop=(o == PASSES - 1),
+                    )
+            prob = sb.tile([P, PACK, NQ], F32, name=f"prob{b}")
+            for r in range(PACK):
+                nc.scalar.activation(prob[:, r, :], scores[r][:], ACT.Sigmoid, bias=kb_cols[:, b, r : r + 1])
+            probs.append(prob)
+            if b == 0:
+                nc.scalar.activation(gate[:], og_raw[:], ACT.Sigmoid)
+
+        for b in range(B):
+            for h in range(HALVES):
+                bh = b * HALVES + h
+                w_woven = sb.tile([P, P, PACK], BF16, name=f"w_woven{bh}", align_bytes=64)
+                nc.vector.tensor_tensor(
+                    w_woven[:].rearrange("p (c i) r -> p c r i", i=4),
+                    probs[b][:, :, h * P : (h + 1) * P].rearrange("p r (c i) -> p c r i", i=4),
+                    vs_cols[b].unsqueeze(1).unsqueeze(3).to_broadcast([P, P // 4, PACK, 4]),
+                    ALU.mult,
+                )
+                w_codes = sb.tile([P, P], U32, name=f"w_codes{bh}", align_bytes=64)
+                w_planes = sb.tile([P, P], U8, name=f"w_planes{bh}", align_bytes=64)
+                nc.vector.quantize_mx(w_codes[:].bitcast(FP8X4), w_planes[:], w_woven[:].rearrange("p q r -> p (q r)"))
+                nc.tensor.matmul_mx(
+                    y_bank[:, bh, :],
+                    lhsT=w_codes[:].bitcast(FP8X4),
+                    lhsT_scale=w_planes[:],
+                    rhs=v_codes[:, b * DV : (b + 1) * DV].bitcast(FP8X4),
+                    rhs_scale=v_planes[:, b * DV : (b + 1) * DV],
+                    start=True,
+                    stop=True,
+                )
+            res = sb.tile([P, HALVES, DV], F32, name=f"res{b}")
+            both = slice(b * HALVES, (b + 1) * HALVES)
+            nc.vector.scalar_tensor_tensor(res[:], y_bank[:, both, :], 1.0 / 16.0, gate[:, both, :], ALU.mult, ALU.mult)
+            nc.sync.dma_start(out[b].rearrange("(h p) e -> p h e", p=P), res[:])

@@ -42,9 +42,15 @@ def tile_attend_sigm_kb_gate_segb2q256n512t2048_kernel(tc, qT, k_words, k_scales
         scale_pool = sb.tile([P, T], U8, name="scale_pool", align_bytes=64)
         kb_pool = sb.tile([P, T], F32, name="kb_pool")
         vs_pool = sb.tile([P, T], F32, name="vs_pool")
+        ident_f32 = sb.tile([P, P], F32, name="ident_f32")
+        ident_bf16 = sb.tile([P, P], BF16, name="ident_bf16")
+        nc.gpsimd.memset(ident_f32[:], 0.0)
         nc.gpsimd.memset(scale_pool[:].bitcast(I32), 0)
-        nc.vector.memset(kb_pool[0:LOADED, :].bitcast(I32), 0)
-        nc.vector.memset(vs_pool[0:LOADED, :].bitcast(I32), 0)
+        make_identity(nc, ident_f32[:], nomemset=True)
+        nc.gpsimd.memset(vs_pool[0:LOADED, :], 0.0)
+        nc.scalar.copy(ident_bf16[:], ident_f32[:])
+        nc.vector.memset(kb_pool[0:LOADED, : SEG - 1], 0.0)
+        nc.vector.memset(kb_pool[0:LOADED, SEG - 1 :], 0.0)
         nc.sync.dma_start(kb_pool[LOADED:P, :], kb[LOADED:P, :])
         nc.sync.dma_start(vs_pool[LOADED:P, :], vs[LOADED:P, :])
         for quad in range(4):
@@ -53,26 +59,30 @@ def tile_attend_sigm_kb_gate_segb2q256n512t2048_kernel(tc, qT, k_words, k_scales
                 k_scales[:, 4 * quad : 4 * quad + 4, :].bitcast(I32),
             )
 
-        v_raw = [sb.tile([P, SEG], F32, name=f"v_raw{b}", tag=f"v_raw{b}") for b in range(B)]
-        for b in range(B):
-            nc.sync.dma_start(v_raw[b][:], vT[:, b * SEG : (b + 1) * SEG])
-        word_pool = [sb.tile([P, T], I32, name=f"word_pool{o}") for o in range(PASSES)]
-        q_raw = [[sb.tile([P, PACK, NQ], F32, name=f"q_raw{b}{o}") for o in range(PASSES)] for b in range(B)]
-        for b in range(B):
+        v_raw = [sb.tile([P, SEG], F32, name=f"v_raw{b}", tag=f"v_raw{b}", align_bytes=64) for b in range(B)]
+        q_raw = [[sb.tile([P, PACK, NQ], F32, name=f"q_raw{b}{o}", tag=f"q_raw{b}{o}", align_bytes=64) for o in range(PASSES)] for b in range(B)]
+        word_pool = [sb.tile([P, T], I32, name=f"word_pool{o}", tag=f"word_pool{o}", align_bytes=64) for o in range(PASSES)]
+
+        def load_queries(b):
             for o in range(PASSES):
                 rows = qT[b, o * P * PACK : (o + 1) * P * PACK, :]
                 nc.sync.dma_start(q_raw[b][o][:], rows.rearrange("(p j) q -> p j q", j=PACK))
-        for b in range(B):
+
+        def load_words(b):
             for o in range(PASSES):
                 words = k_words[o].rearrange("p t r -> p (t r)").bitcast(I32)
                 nc.sync.dma_start(word_pool[o][:, b * SEG : (b + 1) * SEG], words[:, b * SEG : (b + 1) * SEG])
+
+        nc.sync.dma_start(v_raw[0][:, : SEG // 2], vT[:, : SEG // 2])
+        nc.sync.dma_start(v_raw[0][:, SEG // 2 :], vT[:, SEG // 2 : SEG])
+        load_queries(0)
+        nc.sync.dma_start(v_raw[1][:], vT[:, SEG:])
+        load_words(0)
+        load_queries(1)
+        load_words(1)
         og_raw = sb.tile([P, B * HALVES, DV], F32, name="og_raw")
         nc.sync.dma_start(og_raw[:], og.rearrange("b (h p) e -> p (b h) e", p=P))
 
-        ident_f32 = sb.tile([P, P], F32, name="ident_f32")
-        ident_bf16 = sb.tile([P, P], BF16, name="ident_bf16")
-        make_identity(nc, ident_bf16[:])
-        make_identity(nc, ident_f32[:])
 
         def token_columns(pool_tile, label, tag):
             picked = sb.tile([P, PACK, B * P], F32, name=f"{label}_picked")
@@ -99,9 +109,10 @@ def tile_attend_sigm_kb_gate_segb2q256n512t2048_kernel(tc, qT, k_words, k_scales
 
         v_pool = sb.tile([P, T], BF16, name="v_pool", align_bytes=64)
         v_turned = ps.tile([P, B, PACK, DV], BF16, name="v_turned")
-        v_woven = sb.tile([P, B, DV, PACK], BF16, name="v_woven", align_bytes=64)
         for b in range(B):
-            nc.scalar.activation(v_pool[:, b * SEG : (b + 1) * SEG], v_raw[b][:], ACT.Copy)
+            step = SEG // 2 if b == 0 else SEG
+            for c in range(0, SEG, step):
+                nc.scalar.activation(v_pool[:, b * SEG + c : b * SEG + c + step], v_raw[b][:, c : c + step], ACT.Copy)
             v_picked = sb.tile([P, PACK, P], BF16, name=f"v_picked{b}", align_bytes=64)
             nc.scalar.activation(
                 v_picked[:].rearrange("p r (m i) -> p m r i", i=RUN),
@@ -110,31 +121,25 @@ def tile_attend_sigm_kb_gate_segb2q256n512t2048_kernel(tc, qT, k_words, k_scales
             )
             for r in range(PACK):
                 nc.tensor.transpose(v_turned[:, b, r, :], v_picked[:, r, :], ident_bf16[:])
-        kb_cols = sb.tile([P, B, PACK], F32, name="kb_cols", tag="v_raw1")
-        for b in range(B):
-            nc.scalar.activation(kb_cols[:, b, :], kb_turned[b], ACT.Copy)
-        nc.scalar.copy(v_woven[:], v_turned[:].rearrange("p b r e -> p b e r"))
         v_codes = sb.tile([P, B * DV], U32, name="v_codes", align_bytes=64)
         v_planes = sb.tile([P, B * DV], U8, name="v_planes", align_bytes=64)
-        nc.vector.quantize_mx(v_codes[:].bitcast(FP8X4), v_planes[:], v_woven[:].rearrange("p b e r -> p (b e r)"))
 
-        gate = sb.tile([P, B * HALVES, DV], F32, name="gate")
-        y_bank = ps.tile([P, B * HALVES, DV], F32, name="y_bank")
+
+        q_woven = [sb.tile([P, PASSES, NQ, PACK], BF16, name=f"q_woven{b}", align_bytes=64) for b in range(B)]
+        for b in range(B):
+            for o in range(PASSES):
+                nc.scalar.copy(
+                    q_woven[b][:, o].rearrange("p (c i) j -> p c j i", i=4),
+                    q_raw[b][o][:].rearrange("p j (c i) -> p c j i", i=4),
+                )
+
+        kb_cols = [sb.tile([P, PACK], F32, name=f"kb_cols{b}", tag=("v_raw1", "q_raw01")[b], align_bytes=64) for b in range(B)]
+        for b in range(B):
+            nc.scalar.activation(kb_cols[b][:], kb_turned[b], ACT.Copy)
 
         probs = []
         for b in range(B):
-            q_codes, q_planes, keys = [], [], []
-            for o in range(PASSES):
-                q_woven = sb.tile([P, NQ, PACK], BF16, name=f"q_woven{b}{o}", align_bytes=64)
-                nc.scalar.copy(
-                    q_woven[:].rearrange("p (c i) j -> p c j i", i=4),
-                    q_raw[b][o][:].rearrange("p j (c i) -> p c j i", i=4),
-                )
-                codes = sb.tile([P, NQ], U32, name=f"q_codes{b}{o}", align_bytes=64)
-                planes = sb.tile([P, NQ], U8, name=f"q_planes{b}{o}", align_bytes=64)
-                nc.vector.quantize_mx(codes[:].bitcast(FP8X4), planes[:], q_woven[:].rearrange("p q j -> p (q j)"))
-                q_codes.append(codes)
-                q_planes.append(planes)
+            keys = []
             for o in range(PASSES):
                 picked = sb.tile([P, PACK, P], U32, name=f"keys{b}{o}", align_bytes=64)
                 nc.vector.tensor_copy(
@@ -142,6 +147,14 @@ def tile_attend_sigm_kb_gate_segb2q256n512t2048_kernel(tc, qT, k_words, k_scales
                     word_pool[o][:, : (b + 1) * SEG].bitcast(U32).indirect(seq_list(b)),
                 )
                 keys.append(picked)
+                if o == 0:
+                    q_codes = sb.tile([P, PASSES, NQ], U32, name=f"q_codes{b}", tag=("q_codes0", "word_pool0")[b], align_bytes=64)
+                    q_planes = sb.tile([P, PASSES, NQ], U8, name=f"q_planes{b}", align_bytes=64)
+                    nc.vector.quantize_mx(
+                        q_codes[:].rearrange("p o q -> p (o q)").bitcast(FP8X4),
+                        q_planes[:].rearrange("p o q -> p (o q)"),
+                        q_woven[b][:].rearrange("p o q j -> p (o q j)"),
+                    )
             scores = [ps.tile([P, NQ], F32, name=f"scores{b}{r}", tag=f"scores{r}") for r in range(PACK)]
             for o in range(PASSES):
                 for r in range(PACK):
@@ -149,33 +162,40 @@ def tile_attend_sigm_kb_gate_segb2q256n512t2048_kernel(tc, qT, k_words, k_scales
                         scores[r][:],
                         lhsT=keys[o][:, r, :].bitcast(FP8X4),
                         lhsT_scale=k_planes[4 * o :, r, b * P : (b + 1) * P],
-                        rhs=q_codes[o][:].bitcast(FP8X4),
-                        rhs_scale=q_planes[o][:],
+                        rhs=q_codes[:, o, :].bitcast(FP8X4),
+                        rhs_scale=q_planes[:, o, :],
                         start=(o == 0),
                         stop=(o == PASSES - 1),
                     )
-            prob = sb.tile([P, PACK, NQ], F32, name=f"prob{b}")
+            prob = sb.tile([P, PACK, NQ], F32, name=f"prob{b}", tag=("q_raw11", "prob1")[b], align_bytes=64)
             for r in range(PACK):
-                nc.scalar.activation(prob[:, r, :], scores[r][:], ACT.Sigmoid, bias=kb_cols[:, b, r : r + 1])
+                nc.scalar.activation(prob[:, r, :], scores[r][:], ACT.Sigmoid, bias=kb_cols[b][:, r : r + 1])
             probs.append(prob)
             if b == 0:
-                nc.scalar.activation(gate[:], og_raw[:], ACT.Sigmoid)
+                v_woven = sb.tile([P, B, DV, PACK], BF16, name="v_woven", tag="v_raw1", align_bytes=64)
+                nc.scalar.copy(v_woven[:], v_turned[:].rearrange("p b r e -> p b e r"))
+
+        nc.vector.quantize_mx(v_codes[:].bitcast(FP8X4), v_planes[:], v_woven[:].rearrange("p b e r -> p (b e r)"))
+        gate = sb.tile([P, B * HALVES, DV], F32, name="gate", tag="q_raw01", align_bytes=64)
+        nc.scalar.activation(gate[:], og_raw[:], ACT.Sigmoid)
 
         for b in range(B):
+            w_both = sb.tile([P, HALVES, P, PACK], BF16, name=f"w_woven{b}", tag=("word_pool1", "w_woven1")[b], align_bytes=64)
             for h in range(HALVES):
                 bh = b * HALVES + h
-                w_woven = sb.tile([P, P, PACK], BF16, name=f"w_woven{bh}", align_bytes=64)
+                w_woven = w_both[:, h]
                 nc.vector.tensor_tensor(
-                    w_woven[:].rearrange("p (c i) r -> p c r i", i=4),
+                    w_woven.rearrange("p (c i) r -> p c r i", i=4),
                     probs[b][:, :, h * P : (h + 1) * P].rearrange("p r (c i) -> p c r i", i=4),
                     vs_cols[b].unsqueeze(1).unsqueeze(3).to_broadcast([P, P // 4, PACK, 4]),
                     ALU.mult,
                 )
                 w_codes = sb.tile([P, P], U32, name=f"w_codes{bh}", align_bytes=64)
                 w_planes = sb.tile([P, P], U8, name=f"w_planes{bh}", align_bytes=64)
-                nc.vector.quantize_mx(w_codes[:].bitcast(FP8X4), w_planes[:], w_woven[:].rearrange("p q r -> p (q r)"))
+                nc.vector.quantize_mx(w_codes[:].bitcast(FP8X4), w_planes[:], w_woven.rearrange("p q r -> p (q r)"))
+                y = ps.tile([P, DV], F32, name=f"y{bh}", tag=f"scores{bh}")
                 nc.tensor.matmul_mx(
-                    y_bank[:, bh, :],
+                    y[:],
                     lhsT=w_codes[:].bitcast(FP8X4),
                     lhsT_scale=w_planes[:],
                     rhs=v_codes[:, b * DV : (b + 1) * DV].bitcast(FP8X4),
@@ -183,7 +203,6 @@ def tile_attend_sigm_kb_gate_segb2q256n512t2048_kernel(tc, qT, k_words, k_scales
                     start=True,
                     stop=True,
                 )
-            res = sb.tile([P, HALVES, DV], F32, name=f"res{b}")
-            both = slice(b * HALVES, (b + 1) * HALVES)
-            nc.vector.scalar_tensor_tensor(res[:], y_bank[:, both, :], 1.0 / 16.0, gate[:, both, :], ALU.mult, ALU.mult)
-            nc.sync.dma_start(out[b].rearrange("(h p) e -> p h e", p=P), res[:])
+                res = sb.tile([P, DV], F32, name=f"res{bh}")
+                nc.vector.scalar_tensor_tensor(res[:], y[:], 1.0 / 16.0, gate[:, bh, :], ALU.mult, ALU.mult)
+                nc.sync.dma_start(out[b, h * P : (h + 1) * P, :], res[:])

from contextlib import ExitStack

import concourse.mybir as mybir
from concourse.masks import make_identity

B, N, T, D, DV, NQ = 2, 512, 2048, 1024, 128, 256
FLOPS = 2 * B * NQ * N * (D + DV)

F32 = mybir.dt.float32
BF16 = mybir.dt.bfloat16
I32 = mybir.dt.int32
U32 = mybir.dt.uint32
U16 = mybir.dt.uint16
U8 = mybir.dt.uint8
FP8X4 = mybir.dt.float8_e4m3fn_x4
ACT = mybir.ActivationFunctionType
ALU = mybir.AluOpType

P = 128
PACK = 4
PASSES = D // (P * PACK)
SEG = T // B
RUN = 8
LIST_COLS = N // 16
LAST = P - 1
LOADED = 127
HALVES = NQ // P


def tile_attend_sigm_kb_gate_segb2q256n512t2048_kernel(tc, qT, k_words, k_scales, vT, vs, kb, og, offs, out):
    nc = tc.nc
    with ExitStack() as ctx:
        sb = ctx.enter_context(tc.tile_pool(name="sb", bufs=1))
        ps = ctx.enter_context(tc.psum_pool(name="ps", bufs=1))

        offsets = sb.tile([P, B * LIST_COLS], U16, name="offsets")
        nc.sync.dma_start(offsets[:], offs)

        def seq_list(b):
            return offsets[:, b * LIST_COLS : (b + 1) * LIST_COLS]

        scale_pool = sb.tile([P, T], U8, name="scale_pool", align_bytes=64)
        kb_pool = sb.tile([P, T], F32, name="kb_pool")
        vs_pool = sb.tile([P, T], F32, name="vs_pool")
        ident_f32 = sb.tile([P, P], F32, name="ident_f32")
        ident_bf16 = sb.tile([P, P], BF16, name="ident_bf16")
        nc.gpsimd.memset(ident_f32[:], 0.0)
        nc.gpsimd.memset(scale_pool[:].bitcast(I32), 0)
        make_identity(nc, ident_f32[:], nomemset=True)
        nc.gpsimd.memset(vs_pool[0:LOADED, :], 0.0)
        nc.scalar.copy(ident_bf16[:], ident_f32[:])
        nc.vector.memset(kb_pool[0:LOADED, : SEG - 1], 0.0)
        nc.vector.memset(kb_pool[0:LOADED, SEG - 1 :], 0.0)
        nc.sync.dma_start(kb_pool[LOADED:P, :], kb[LOADED:P, :])
        nc.sync.dma_start(vs_pool[LOADED:P, :], vs[LOADED:P, :])
        for quad in range(4):
            nc.sync.dma_start(
                scale_pool[32 * quad : 32 * quad + 4 * PASSES, :].bitcast(I32),
                k_scales[:, 4 * quad : 4 * quad + 4, :].bitcast(I32),
            )

        v_raw = [sb.tile([P, SEG], F32, name=f"v_raw{b}", tag=f"v_raw{b}", align_bytes=64) for b in range(B)]
        q_raw = [[sb.tile([P, PACK, NQ], F32, name=f"q_raw{b}{o}", tag=f"q_raw{b}{o}", align_bytes=64) for o in range(PASSES)] for b in range(B)]
        word_pool = [sb.tile([P, T], I32, name=f"word_pool{o}", tag=f"word_pool{o}", align_bytes=64) for o in range(PASSES)]

        def load_queries(b):
            for o in range(PASSES):
                rows = qT[b, o * P * PACK : (o + 1) * P * PACK, :]
                nc.sync.dma_start(q_raw[b][o][:], rows.rearrange("(p j) q -> p j q", j=PACK))

        def load_words(b):
            for o in range(PASSES):
                words = k_words[o].rearrange("p t r -> p (t r)").bitcast(I32)
                nc.sync.dma_start(word_pool[o][:, b * SEG : (b + 1) * SEG], words[:, b * SEG : (b + 1) * SEG])

        nc.sync.dma_start(v_raw[0][:, : SEG // 2], vT[:, : SEG // 2])
        nc.sync.dma_start(v_raw[0][:, SEG // 2 :], vT[:, SEG // 2 : SEG])
        load_queries(0)
        nc.sync.dma_start(v_raw[1][:], vT[:, SEG:])
        load_words(0)
        load_queries(1)
        load_words(1)
        og_raw = sb.tile([P, B * HALVES, DV], F32, name="og_raw")
        nc.sync.dma_start(og_raw[:], og.rearrange("b (h p) e -> p (b h) e", p=P))


        def token_columns(pool_tile, label, tag):
            picked = sb.tile([P, PACK, B * P], F32, name=f"{label}_picked")
            dealt = picked[:].bitcast(U32).rearrange("p r (m i) -> p m r i", i=RUN)
            nc.vector.tensor_copy(dealt, pool_tile[:].bitcast(U32).indirect(offsets[:]))
            cols = []
            for b in range(B):
                turned = ps.tile([P, PACK, P], F32, name=f"{label}_turned{b}", tag=f"{tag}{b}")
                for r in range(PACK):
                    nc.tensor.transpose(turned[:, r, :], picked[:, r, b * P : (b + 1) * P], ident_f32[:])
                cols.append(turned[:, :, LAST])
            return cols

        kb_turned = token_columns(kb_pool, "kb", "scores")
        vs_cols = token_columns(vs_pool, "vs", "vs_bank")

        scale_picked = sb.tile([P, B * N], U8, name="scale_picked", align_bytes=64)
        nc.vector.tensor_copy(scale_picked[:], scale_pool[:].indirect(offsets[:]))
        k_planes = sb.tile([P, PACK, B * P], U8, name="k_planes", align_bytes=64)
        nc.vector.tensor_copy(
            k_planes[:].bitcast(I32).rearrange("p r (m w) -> p m r w", w=RUN // 4),
            scale_picked[:].bitcast(I32).rearrange("p (m r w) -> p m r w", r=PACK, w=RUN // 4),
        )

        v_pool = sb.tile([P, T], BF16, name="v_pool", align_bytes=64)
        v_turned = ps.tile([P, B, PACK, DV], BF16, name="v_turned")
        for b in range(B):
            step = SEG // 2 if b == 0 else SEG
            for c in range(0, SEG, step):
                nc.scalar.activation(v_pool[:, b * SEG + c : b * SEG + c + step], v_raw[b][:, c : c + step], ACT.Copy)
            v_picked = sb.tile([P, PACK, P], BF16, name=f"v_picked{b}", align_bytes=64)
            nc.scalar.activation(
                v_picked[:].rearrange("p r (m i) -> p m r i", i=RUN),
                v_pool[:, : (b + 1) * SEG].indirect(seq_list(b)),
                ACT.Copy,
            )
            for r in range(PACK):
                nc.tensor.transpose(v_turned[:, b, r, :], v_picked[:, r, :], ident_bf16[:])
        v_codes = sb.tile([P, B * DV], U32, name="v_codes", align_bytes=64)
        v_planes = sb.tile([P, B * DV], U8, name="v_planes", align_bytes=64)


        q_woven = [sb.tile([P, PASSES, NQ, PACK], BF16, name=f"q_woven{b}", align_bytes=64) for b in range(B)]
        for b in range(B):
            for o in range(PASSES):
                nc.scalar.copy(
                    q_woven[b][:, o].rearrange("p (c i) j -> p c j i", i=4),
                    q_raw[b][o][:].rearrange("p j (c i) -> p c j i", i=4),
                )

        kb_cols = [sb.tile([P, PACK], F32, name=f"kb_cols{b}", tag=("v_raw1", "q_raw01")[b], align_bytes=64) for b in range(B)]
        for b in range(B):
            nc.scalar.activation(kb_cols[b][:], kb_turned[b], ACT.Copy)

        probs = []
        for b in range(B):
            keys = []
            for o in range(PASSES):
                picked = sb.tile([P, PACK, P], U32, name=f"keys{b}{o}", align_bytes=64)
                nc.vector.tensor_copy(
                    picked[:].rearrange("p r (m i) -> p m r i", i=RUN),
                    word_pool[o][:, : (b + 1) * SEG].bitcast(U32).indirect(seq_list(b)),
                )
                keys.append(picked)
                if o == 0:
                    q_codes = sb.tile([P, PASSES, NQ], U32, name=f"q_codes{b}", tag=("q_codes0", "word_pool0")[b], align_bytes=64)
                    q_planes = sb.tile([P, PASSES, NQ], U8, name=f"q_planes{b}", align_bytes=64)
                    nc.vector.quantize_mx(
                        q_codes[:].rearrange("p o q -> p (o q)").bitcast(FP8X4),
                        q_planes[:].rearrange("p o q -> p (o q)"),
                        q_woven[b][:].rearrange("p o q j -> p (o q j)"),
                    )
            scores = [ps.tile([P, NQ], F32, name=f"scores{b}{r}", tag=f"scores{r}") for r in range(PACK)]
            for o in range(PASSES):
                for r in range(PACK):
                    nc.tensor.matmul_mx(
                        scores[r][:],
                        lhsT=keys[o][:, r, :].bitcast(FP8X4),
                        lhsT_scale=k_planes[4 * o :, r, b * P : (b + 1) * P],
                        rhs=q_codes[:, o, :].bitcast(FP8X4),
                        rhs_scale=q_planes[:, o, :],
                        start=(o == 0),
                        stop=(o == PASSES - 1),
                    )
            prob = sb.tile([P, PACK, NQ], F32, name=f"prob{b}", tag=("q_raw11", "prob1")[b], align_bytes=64)
            for r in range(PACK):
                nc.scalar.activation(prob[:, r, :], scores[r][:], ACT.Sigmoid, bias=kb_cols[b][:, r : r + 1])
            probs.append(prob)
            if b == 0:
                v_woven = sb.tile([P, B, DV, PACK], BF16, name="v_woven", tag="v_raw1", align_bytes=64)
                nc.scalar.copy(v_woven[:], v_turned[:].rearrange("p b r e -> p b e r"))

        nc.vector.quantize_mx(v_codes[:].bitcast(FP8X4), v_planes[:], v_woven[:].rearrange("p b e r -> p (b e r)"))
        gate = sb.tile([P, B * HALVES, DV], F32, name="gate", tag="q_raw01", align_bytes=64)
        nc.scalar.activation(gate[:], og_raw[:], ACT.Sigmoid)

        for b in range(B):
            w_both = sb.tile([P, HALVES, P, PACK], BF16, name=f"w_woven{b}", tag=("word_pool1", "w_woven1")[b], align_bytes=64)
            for h in range(HALVES):
                bh = b * HALVES + h
                w_woven = w_both[:, h]
                nc.vector.tensor_tensor(
                    w_woven.rearrange("p (c i) r -> p c r i", i=4),
                    probs[b][:, :, h * P : (h + 1) * P].rearrange("p r (c i) -> p c r i", i=4),
                    vs_cols[b].unsqueeze(1).unsqueeze(3).to_broadcast([P, P // 4, PACK, 4]),
                    ALU.mult,
                )
                w_codes = sb.tile([P, P], U32, name=f"w_codes{bh}", align_bytes=64)
                w_planes = sb.tile([P, P], U8, name=f"w_planes{bh}", align_bytes=64)
                nc.vector.quantize_mx(w_codes[:].bitcast(FP8X4), w_planes[:], w_woven.rearrange("p q r -> p (q r)"))
                y = ps.tile([P, DV], F32, name=f"y{bh}", tag=f"scores{bh}")
                nc.tensor.matmul_mx(
                    y[:],
                    lhsT=w_codes[:].bitcast(FP8X4),
                    lhsT_scale=w_planes[:],
                    rhs=v_codes[:, b * DV : (b + 1) * DV].bitcast(FP8X4),
                    rhs_scale=v_planes[:, b * DV : (b + 1) * DV],
                    start=True,
                    stop=True,
                )
                res = sb.tile([P, DV], F32, name=f"res{bh}")
                nc.vector.scalar_tensor_tensor(res[:], y[:], 1.0 / 16.0, gate[:, bh, :], ALU.mult, ALU.mult)
                nc.sync.dma_start(out[b, h * P : (h + 1) * P, :], res[:])
